import numpy as np
import ml_dtypes


def mxq(x, axis, fmt="e4m3"):
    dtype, down = {"e4m3": (ml_dtypes.float8_e4m3fn, 7), "e5m2": (ml_dtypes.float8_e5m2, 14)}[fmt]
    v = np.moveaxis(np.asarray(x, np.float32).astype(ml_dtypes.bfloat16).astype(np.float64), axis, -1)
    blocks = v.reshape(v.shape[:-1] + (-1, 32))
    amax = np.abs(blocks).max(-1, keepdims=True)
    byte = np.maximum(np.where(amax > 0, np.frexp(amax)[1] - 1 + 127, 0) - down, 1)
    scale = np.exp2(byte - 127.0)
    codes = (blocks / scale).astype(np.float32).astype(dtype).astype(np.float64)
    return np.moveaxis((codes * scale).reshape(v.shape), -1, axis)


WIDE = False


def mx_kscale(k):
    if not WIDE:
        return np.ones(k)
    levels = np.array([10, -10, 5, -5, 0])
    if k % 512:
        return np.exp2(np.random.permutation(np.resize(levels, k // 32))).repeat(32)
    a = np.empty((k // 512, 16))
    for p in range(k // 512):
        a[p, :8] = np.random.permutation(np.resize(levels, 8))
        for g in range(8):
            far = levels[np.abs(levels - a[p, g]) >= 10]
            a[p, g + 8] = far[np.random.randint(len(far))]
    return np.exp2(a.ravel()).repeat(32)


def f64(x):
    return np.asarray(x).astype(np.float64)


def striped(idx):
    return np.tile(idx.reshape(-1, 16).T, (8, 1)).astype(np.uint16)


def unstriped(offs):
    return offs[:16].T.reshape(-1).astype(np.int64)


def striped8(idx):
    return np.concatenate([x.reshape(-1, 16).T for x in idx]).astype(np.uint16)


def runs(offs, k):
    lists = np.stack([offs[16 * r : 16 * r + 16].T.reshape(-1) for r in range(8)]).astype(np.int64)
    return lists[np.arange(k) % 512 // 64]


def pack_weight(w):
    k, n = w.shape
    w = f64(np.asarray(w, np.float32).astype(ml_dtypes.bfloat16)).reshape(k // 32, 32, n)
    amax = np.abs(w).max(1)
    byte = np.clip(np.where(amax > 0, np.frexp(amax)[1] - 1 + 127 - 7, 1), 1, 254)
    scaled = (w * np.exp2(127.0 - byte)[:, None, :]).reshape(k, n).astype(np.float32)
    words = np.ascontiguousarray(scaled.reshape(k // 512, 128, 4, n).transpose(0, 1, 3, 2)).astype(ml_dtypes.float8_e4m3fn).view(np.uint8)
    return words, np.ascontiguousarray(byte.astype(np.uint8).reshape(k // 512, 16, n))


def unpack_weight(words, scales):
    g, p, n, _ = words.shape
    vals = np.ascontiguousarray(words).view(ml_dtypes.float8_e4m3fn).astype(np.float64) * np.repeat(np.exp2(scales.astype(np.float64) - 127.0), 8, axis=1)[..., None]
    return vals.transpose(0, 1, 3, 2).reshape(g * 512, n)


E2M1 = np.array([0.0, 0.5, 1.0, 1.5, 2.0, 3.0, 4.0, 6.0, -0.0, -0.5, -1.0, -1.5, -2.0, -3.0, -4.0, -6.0])


def pack_fp4(w):
    k, n = w.shape
    w = f64(np.asarray(w, np.float32).astype(ml_dtypes.bfloat16)).reshape(k // 32, 32, n)
    amax = np.abs(w).max(1)
    mant, ex = np.frexp(amax / 6.0)
    byte = np.clip(np.where(amax > 0, np.where(mant > 0.5, ex, ex - 1) + 127, 1), 1, 254)
    scaled = (w * np.exp2(127.0 - byte)[:, None, :]).reshape(k, n).astype(np.float32)
    c = np.ascontiguousarray(scaled.reshape(k // 512, 128, 4, n).transpose(0, 1, 3, 2)).astype(ml_dtypes.float4_e2m1fn).view(np.uint8) & 0xF
    words = (c[..., 0::2] | (c[..., 1::2] << 4)).reshape(k // 512, 128, 2 * n)
    return np.ascontiguousarray(words), np.ascontiguousarray(byte.astype(np.uint8).reshape(k // 512, 16, n))


def unpack_fp4(words, scales):
    g, _, n = scales.shape
    words = np.ascontiguousarray(words).reshape(g, 128, n, 2)
    nib = np.empty((g, 128, n, 4), np.uint8)
    nib[..., 0::2] = words & 0xF
    nib[..., 1::2] = words >> 4
    vals = E2M1[nib] * np.repeat(np.exp2(scales.astype(np.float64) - 127.0), 8, axis=1)[..., None]
    return vals.transpose(0, 1, 3, 2).reshape(g * 512, n)


def planes(y):
    n, m = y.shape
    v = y.astype(np.float32).astype(ml_dtypes.bfloat16).astype(np.float64).reshape(n // 32, 32, m)
    top = np.abs(v).max(1)
    byte = np.clip(np.where(top > 0, np.frexp(top)[1] - 1 + 127 - 7, 1), 1, 254)
    codes = (v * np.exp2(127.0 - byte)[:, None, :]).reshape(n, m).astype(np.float32).astype(ml_dtypes.float8_e4m3fn).view(np.uint8)
    words = codes.reshape(n // 512, 128, 4, m).transpose(0, 1, 3, 2)
    return np.ascontiguousarray(words), np.ascontiguousarray(byte.astype(np.uint8).reshape(n // 512, 16, m))


K, T, S, N, H, W = 512, 2048, 512, 512, 512, 256


def setup_inputs():
    n = np.random.standard_normal
    s = mx_kscale(K)[:, None]
    u = mx_kscale(H)
    packed_xT = pack_weight(n((K, T)) * s)
    packed_w1 = pack_fp4(n((K, H)) / np.sqrt(K) / s)
    packed_w2 = pack_fp4(n((H, N)) / np.sqrt(2 * H) / u[:, None])
    packed_w3 = pack_fp4(n((H, N)) / np.sqrt(2 * H) / u[:, None])
    perm = np.stack([np.random.permutation(S) for _ in range(8)])
    return {
        "x_words": packed_xT[0],
        "x_scales": packed_xT[1],
        "w1_words": packed_w1[0],
        "w1_scales": packed_w1[1],
        "gn": (np.random.uniform(0.5, 1.5, (H, 1)) * u[:, None]).astype(np.float32),
        "gm": (np.random.uniform(0.5, 1.5, (H, 1)) * u[:, None]).astype(np.float32),
        "w2_words": packed_w2[0],
        "w2_scales": packed_w2[1],
        "w3_words": packed_w3[0],
        "w3_scales": packed_w3[1],
        "offs": striped(np.random.permutation(T)[:S]),
        "n1": striped8(perm[:, :W]),
        "n2": striped8(perm[:, W:]),
        "n3": striped8(np.stack([np.random.permutation(S) for _ in range(8)])),
        "n4": striped8(np.stack([np.random.permutation(S) for _ in range(8)])),
        "n5": striped8(np.stack([np.random.permutation(S) for _ in range(8)])),
        "n6": striped8(np.stack([np.random.permutation(S) for _ in range(8)])),
    }


def reference(x_words, x_scales, w1_words, w1_scales, gn, gm, w2_words, w2_scales, w3_words, w3_scales, offs, n1, n2, n3, n4, n5, n6):
    xq = unpack_weight(x_words, x_scales)[:, unstriped(offs)]
    y = unpack_fp4(w1_words, w1_scales).T @ xq
    pa = y[np.arange(H)[:, None], runs(n1, H)]
    pb = y[np.arange(H)[:, None], runs(n2, H)]
    rb = pa * pb
    ra = pa + pb
    ds = np.zeros((H, S))
    ds[np.arange(H)[:, None], runs(n1, H)] = ra
    dt = ds.copy()
    dt[np.arange(H)[:, None], runs(n2, H)] = rb
    z = f64(gn) * dt
    z2 = f64(gm) * (y - (y[np.arange(H)[:, None], runs(n3, H)]))
    h = unpack_fp4(w2_words, w2_scales).T @ mxq(z, 0, "e4m3") + unpack_fp4(w3_words, w3_scales).T @ mxq(z2, 0, "e4m3")
    b1 = h[np.arange(N)[:, None], runs(n4, N)]
    b2 = h[np.arange(N)[:, None], runs(n5, N)]
    b3 = h[np.arange(N)[:, None], runs(n6, N)]
    out_0 = np.maximum(np.maximum(b1, b2), b3) - (0.5 * (np.maximum(np.minimum(b1, b2), np.minimum(np.maximum(b1, b2), b3))))
    return (out_0,) + planes(out_0)

@@ -1,0 +1,275 @@
+from contextlib import ExitStack
+
+import concourse.mybir as mybir
+from concourse.masks import make_identity
+
+K, T, S, N, H, W = 512, 2048, 512, 512, 512, 256
+FLOPS = 2 * (K * H * S + 2 * H * N * S)
+
+F32 = mybir.dt.float32
+BF16 = mybir.dt.bfloat16
+I32 = mybir.dt.int32
+U32 = mybir.dt.uint32
+U16 = mybir.dt.uint16
+U8 = mybir.dt.uint8
+FP8X4 = mybir.dt.float8_e4m3fn_x4
+FP4X4 = mybir.dt.float4_e2m1fn_x4
+ALU = mybir.AluOpType
+ACT = mybir.ActivationFunctionType
+
+P = 128
+R = 4
+CHUNKS = ((0, 256), (256, 128), (384, 128))
+UNIT = 128
+
+
+def tile_picked_joinbonddiftop2_none_po_kernel(
+    tc, x_words, x_scales, w1_words, w1_scales, gn, gm, w2_words, w2_scales, w3_words, w3_scales,
+    offs, n1, n2, n3, n4, n5, n6, out_0, out_1, out_2,
+):
+    nc = tc.nc
+    with ExitStack() as ctx:
+        lists = ctx.enter_context(tc.tile_pool(name="lists", bufs=1))
+        keep = ctx.enter_context(tc.tile_pool(name="keep", bufs=1))
+        psum = ctx.enter_context(tc.psum_pool(name="psum", bufs=1))
+
+        def load_list(name, src):
+            tile = lists.tile(list(src.shape), U16, name=name)
+            nc.sync.dma_start(tile[:], src)
+            return tile
+
+        def load_scale_rows(queue, tile, src):
+            for q in range(4):
+                queue.dma_start(tile[32 * q : 32 * q + 4, :].bitcast(I32), src[0, 4 * q : 4 * q + 4, :].bitcast(I32))
+
+        def zeroed_plane(engine, name, width):
+            tile = keep.tile([P, width], U8, name=name, align_bytes=64)
+            engine.memset(tile[:].bitcast(I32), 0)
+            return tile
+
+        def load_words(name, src):
+            tile = keep.tile([P, 2 * H], U8, name=name, align_bytes=64)
+            nc.sync.dma_start(tile[:].bitcast(I32), src[0].bitcast(I32))
+            return tile
+
+        def deal_words(name, raw):
+            tile = keep.tile([P, 2 * H], U8, name=name, align_bytes=64)
+            nc.vector.tensor_copy(
+                tile[:].rearrange("p (t m b) -> p t m b", t=R, b=2), raw[:].rearrange("p (m t b) -> p t m b", t=R, b=2)
+            )
+            return tile
+
+        def deal_scales(name, raw):
+            tile = keep.tile([P, H], U8, name=name, align_bytes=64)
+            nc.vector.tensor_copy(tile[:].rearrange("p (t m) -> p t m", t=R), raw[:].rearrange("p (m t) -> p t m", t=R))
+            return tile
+
+        def product(bank, words, scales, t, codes, planes, start, stop):
+            nc.tensor.matmul_mx(
+                out=bank[:],
+                lhsT=words[:, 2 * P * t : 2 * P * (t + 1)].bitcast(FP4X4),
+                lhsT_scale=scales[:, P * t : P * (t + 1)],
+                rhs=codes[:].bitcast(FP8X4),
+                rhs_scale=planes[:],
+                start=start,
+                stop=stop,
+            )
+
+        xs_all = zeroed_plane(nc.gpsimd, "xs_all", T)
+        w1s_raw = zeroed_plane(nc.gpsimd, "w1s_raw", H)
+        w2s_raw = zeroed_plane(nc.gpsimd, "w2s_raw", N)
+        w3s_raw = zeroed_plane(nc.gpsimd, "w3s_raw", N)
+
+        w1w_raw = load_words("w1w_raw", w1_words)
+        load_scale_rows(nc.sync, xs_all, x_scales)
+        offs_sb = load_list("offs_sb", offs)
+        xw_all = keep.tile([P, T], I32, name="xw_all", align_bytes=64)
+        nc.sync.dma_start(xw_all[:], x_words[0].rearrange("p n t -> p (n t)").bitcast(I32))
+        load_scale_rows(nc.sync, w1s_raw, w1_scales)
+        gm_sb = keep.tile([P, R], F32, name="gm_sb")
+        nc.sync.dma_start(gm_sb[:], gm.rearrange("(p t) o -> p (t o)", t=R))
+        n1_sb = load_list("n1_sb", n1)
+        n2_sb = load_list("n2_sb", n2)
+        w2w_raw = load_words("w2w_raw", w2_words)
+        w3w_raw = load_words("w3w_raw", w3_words)
+        gn_sb = keep.tile([P, R], F32, name="gn_sb")
+        nc.sync.dma_start(gn_sb[:], gn.rearrange("(p t) o -> p (t o)", t=R))
+        load_scale_rows(nc.sync, w2s_raw, w2_scales)
+        load_scale_rows(nc.sync, w3s_raw, w3_scales)
+        n3_sb = load_list("n3_sb", n3)
+        n4_sb = load_list("n4_sb", n4)
+        n5_sb = load_list("n5_sb", n5)
+        n6_sb = load_list("n6_sb", n6)
+
+        ident = keep.tile([P, P], F32, name="ident")
+        make_identity(nc, ident[:])
+        neg_gm = keep.tile([P, R], F32, name="neg_gm")
+        nc.scalar.activation(neg_gm[:], gm_sb[:], ACT.Copy, scale=-1.0)
+
+        xs = keep.tile([P, S], U8, name="xs", align_bytes=64)
+        nc.vector.tensor_copy(xs[:], xs_all[:].indirect(offs_sb[:]))
+        w1w = deal_words("w1w", w1w_raw)
+        xw = keep.tile([P, S], U32, name="xw", align_bytes=64)
+        nc.vector.tensor_copy(xw[:], xw_all[:].bitcast(U32).indirect(offs_sb[:]))
+        w1s = deal_scales("w1s", w1s_raw)
+
+        y_banks = []
+        for t in range(R):
+            bank = psum.tile([P, S], F32, name="y_bank%d" % t, tag="bank", bufs=8)
+            product(bank, w1w, w1s, t, xw, xs, True, True)
+            y_banks.append(bank)
+        y = []
+        for t in range(R):
+            tile = keep.tile([P, S], F32, name="y%d" % t)
+            nc.scalar.copy(tile[:], y_banks[t][:])
+            y.append(tile)
+        w2w = deal_words("w2w", w2w_raw)
+        w3w = deal_words("w3w", w3w_raw)
+
+        neg_gy = []
+        pos_gy = [
+            keep.tile([P, R, width], F32, name="pos_gy%d" % c, tag="stage%d" % (c + 1)) for c, (c0, width) in enumerate(CHUNKS)
+        ]
+        for t in range(R):
+            tile = keep.tile([P, S], F32, name="neg_gy%d" % t)
+            nc.scalar.activation(tile[:], y_banks[t][:], ACT.Copy, scale=neg_gm[:, t : t + 1])
+            neg_gy.append(tile)
+            for c, (c0, width) in enumerate(CHUNKS):
+                nc.scalar.activation(
+                    pos_gy[c][:, t, :], y_banks[t][:, c0 : c0 + width], ACT.Copy, scale=gm_sb[:, t : t + 1]
+                )
+
+        z_bf = keep.tile([P, S, R], BF16, name="z_bf", align_bytes=64)
+        for pair in range(R // 2):
+            ts = (2 * pair, 2 * pair + 1)
+            picked = keep.tile([P, 2, 2, W], F32, name="picked%d" % pair, tag="stage0" if pair else "picked")
+            dt = {}
+            for t in ts:
+                dt[t] = keep.tile([P, S], F32, name="dt%d" % t)
+                nc.vector.tensor_copy(picked[:, t % 2, 0, :], y[t][:].indirect(n1_sb[:]))
+                nc.vector.tensor_copy(picked[:, t % 2, 1, :], y[t][:].indirect(n2_sb[:]))
+            for t in ts:
+                nc.vector.tensor_tensor(dt[t][:].indirect(n1_sb[:]), picked[:, t % 2, 0, :], picked[:, t % 2, 1, :], ALU.add)
+            for t in ts:
+                nc.vector.tensor_tensor(dt[t][:].indirect(n2_sb[:]), picked[:, t % 2, 0, :], picked[:, t % 2, 1, :], ALU.mult)
+                nc.scalar.activation(z_bf[:, :, t], dt[t][:], ACT.Copy, scale=gn_sb[:, t : t + 1])
+        w2s = deal_scales("w2s", w2s_raw)
+        w3s = deal_scales("w3s", w3s_raw)
+
+        z_codes = keep.tile([P, S], U32, name="z_codes", align_bytes=64)
+        z_scales = keep.tile([P, S], U8, name="z_scales", align_bytes=64)
+        z2_codes = keep.tile([P, S], U32, name="z2_codes", align_bytes=64)
+        z2_scales = keep.tile([P, S], U8, name="z2_scales", align_bytes=64)
+        z2_bf = []
+        for c, (c0, width) in enumerate(CHUNKS):
+            z2 = keep.tile([P, R, width], F32, name="z2_%d" % c, tag="stage%d" % c)
+            for t in range(R):
+                nc.vector.tensor_tensor(
+                    z2[:, t, :],
+                    neg_gy[t][:].indirect(n3_sb[:, c0 // 16 : (c0 + width) // 16]),
+                    pos_gy[c][:, t, :],
+                    ALU.add,
+                )
+            rounded = keep.tile([P, width, R], BF16, name="z2_bf%d" % c, align_bytes=64)
+            if c < len(CHUNKS) - 1:
+                nc.scalar.copy(rounded[:], z2[:].rearrange("p t j -> p j t"))
+            else:
+                nc.vector.tensor_copy(rounded[:], z2[:].rearrange("p t j -> p j t"))
+            z2_bf.append(rounded)
+            if c == 0:
+                nc.vector.quantize_mx(z_codes[:].bitcast(FP8X4), z_scales[:], z_bf[:].rearrange("p j t -> p (j t)"))
+        for c, (c0, width) in enumerate(CHUNKS):
+            nc.vector.quantize_mx(
+                z2_codes[:, c0 : c0 + width].bitcast(FP8X4),
+                z2_scales[:, c0 : c0 + width],
+                z2_bf[c][:].rearrange("p j t -> p (j t)"),
+            )
+
+        h_banks = []
+        for t in range(R):
+            bank = psum.tile([P, S], F32, name="h_bank%d" % t, tag="bank", bufs=8)
+            product(bank, w2w, w2s, t, z_codes, z_scales, True, False)
+            h_banks.append(bank)
+        neg_h, pos_h = [], []
+        for t in range(R):
+            product(h_banks[t], w3w, w3s, t, z2_codes, z2_scales, False, True)
+            tile = keep.tile([P, S], F32, name="neg_h%d" % t)
+            nc.scalar.activation(tile[:], h_banks[t][:], ACT.Copy, scale=-1.0)
+            neg_h.append(tile)
+            tile = keep.tile([P, S], F32, name="pos_h%d" % t)
+            nc.scalar.copy(tile[:], h_banks[t][:])
+            pos_h.append(tile)
+
+        out_rows = out_0.rearrange("(p t) j -> p t j", t=R)
+        out_words = out_1[0].rearrange("p n t -> p (n t)").bitcast(I32)
+        o_codes = keep.tile([P, S], I32, name="o_codes", align_bytes=64)
+        o_scales = keep.tile([P, S], U8, name="o_scales", align_bytes=64)
+
+        def hand_out(u0, result, rounded):
+            cols = slice(u0, u0 + UNIT)
+            nc.sync.dma_start(out_rows[:, :, cols], result[:])
+            nc.vector.quantize_mx(
+                o_codes[:, cols].bitcast(FP8X4), o_scales[:, cols], rounded[:].rearrange("p j t -> p (j t)")
+            )
+            nc.sync.dma_start(out_words[:, cols], o_codes[:, cols])
+
+        def summed_transposes(bank, terms):
+            for t in range(R):
+                for i, term in enumerate(terms):
+                    nc.tensor.matmul(
+                        bank[:, t, :], term[:, t, :], ident[:],
+                        start=(i == 0), stop=(i == len(terms) - 1), is_transpose=True,
+                    )
+
+        waiting = []
+        for c, (c0, width) in enumerate(CHUNKS):
+            cols16 = slice(c0 // 16, (c0 + width) // 16)
+            nb1 = keep.tile([P, R, width], F32, name="nb1_%d" % c, tag="nb1")
+            nb2 = keep.tile([P, R, width], F32, name="nb2_%d" % c, tag="nb2")
+            b3 = keep.tile([P, R, width], F32, name="b3_%d" % c, tag="b3")
+            for t in range(R):
+                nc.vector.tensor_copy(nb1[:, t, :], neg_h[t][:].indirect(n4_sb[:, cols16]))
+                nc.vector.tensor_copy(nb2[:, t, :], neg_h[t][:].indirect(n5_sb[:, cols16]))
+                nc.vector.tensor_copy(b3[:, t, :], pos_h[t][:].indirect(n6_sb[:, cols16]))
+            for args in waiting:
+                hand_out(*args)
+            waiting = []
+            for u in range(width // UNIT):
+                u0 = c0 + u * UNIT
+                cols = slice(u * UNIT, (u + 1) * UNIT)
+                neg_lo = keep.tile([P, R, UNIT], F32, name="neg_lo%d" % u0)
+                neg_hi = keep.tile([P, R, UNIT], F32, name="neg_hi%d" % u0)
+                rival = keep.tile([P, R, UNIT], F32, name="rival%d" % u0)
+                nc.vector.tensor_tensor(neg_lo[:], nb1[:, :, cols], nb2[:, :, cols], ALU.max)
+                nc.vector.tensor_tensor(neg_hi[:], nb1[:, :, cols], nb2[:, :, cols], ALU.min)
+                nc.vector.scalar_tensor_tensor(rival[:], neg_lo[:], -1.0, b3[:, :, cols], ALU.mult, ALU.max)
+                result = keep.tile([P, R, UNIT], F32, name="result%d" % u0)
+                rounded = keep.tile([P, UNIT, R], BF16, name="rounded%d" % u0, align_bytes=64)
+                if c < len(CHUNKS) - 1:
+                    hi_bank = psum.tile([P, R, UNIT], F32, name="hi_bank%d" % u0, tag="bank", bufs=8)
+                    gap_bank = psum.tile([P, R, UNIT], F32, name="gap_bank%d" % u0, tag="bank", bufs=8)
+                    sum_bank = psum.tile([P, R, UNIT], F32, name="sum_bank%d" % u0, tag="bank", bufs=8)
+                    summed_transposes(hi_bank, [neg_hi])
+                    summed_transposes(gap_bank, [neg_hi, rival])
+                    half_hi = keep.tile([P, R, UNIT], F32, name="half_hi%d" % u0)
+                    above = keep.tile([P, R, UNIT], F32, name="above%d" % u0)
+                    below = keep.tile([P, R, UNIT], F32, name="below%d" % u0)
+                    nc.scalar.activation(half_hi[:], hi_bank[:], ACT.Copy, scale=-0.5)
+                    nc.scalar.activation(above[:], gap_bank[:], ACT.Relu)
+                    nc.scalar.activation(below[:], gap_bank[:], ACT.Relu, scale=-0.5)
+                    summed_transposes(sum_bank, [half_hi, above, below])
+                    nc.scalar.copy(result[:], sum_bank[:])
+                    nc.scalar.copy(rounded[:], sum_bank[:].rearrange("p t j -> p j t"))
+                    waiting.append((u0, result, rounded))
+                else:
+                    first = keep.tile([P, R, UNIT], F32, name="first")
+                    second = keep.tile([P, R, UNIT], F32, name="second")
+                    nc.vector.scalar_tensor_tensor(first[:], neg_hi[:], 0.5, rival[:], ALU.mult, ALU.add)
+                    nc.vector.scalar_tensor_tensor(second[:], rival[:], -0.5, neg_hi[:], ALU.mult, ALU.subtract)
+                    nc.vector.tensor_tensor(result[:], first[:], second[:], ALU.max)
+                    nc.vector.tensor_copy(rounded[:], result[:].rearrange("p t j -> p j t"))
+                    hand_out(u0, result, rounded)
+
+        for q in range(4):
+            queue = nc.scalar if q % 2 else nc.sync
+            queue.dma_start(out_2[0, 4 * q : 4 * q + 4, :].bitcast(I32), o_scales[32 * q : 32 * q + 4, :].bitcast(I32))

@@ -43,24 +43,24 @@ def tile_picked_joinbonddiftop2_none_po_kernel(
                 queue.dma_start(tile[32 * q : 32 * q + 4, :].bitcast(I32), src[0, 4 * q : 4 * q + 4, :].bitcast(I32))
 
         def zeroed_plane(engine, name, width):
-            tile = keep.tile([P, width], U8, name=name, align_bytes=64)
+            tile = keep.tile([P, width], U8, name=name, tag=name, align_bytes=64)
             engine.memset(tile[:].bitcast(I32), 0)
             return tile
 
         def load_words(name, src):
-            tile = keep.tile([P, 2 * H], U8, name=name, align_bytes=64)
+            tile = keep.tile([P, 2 * H], U8, name=name, tag=name, align_bytes=64)
             nc.sync.dma_start(tile[:].bitcast(I32), src[0].bitcast(I32))
             return tile
 
-        def deal_words(name, raw):
-            tile = keep.tile([P, 2 * H], U8, name=name, align_bytes=64)
+        def deal_words(name, raw, tag):
+            tile = keep.tile([P, 2 * H], U8, name=name, tag=tag, align_bytes=64)
             nc.vector.tensor_copy(
                 tile[:].rearrange("p (t m b) -> p t m b", t=R, b=2), raw[:].rearrange("p (m t b) -> p t m b", t=R, b=2)
             )
             return tile
 
-        def deal_scales(name, raw):
-            tile = keep.tile([P, H], U8, name=name, align_bytes=64)
+        def deal_scales(name, raw, tag):
+            tile = keep.tile([P, H], U8, name=name, tag=tag, align_bytes=64)
             nc.vector.tensor_copy(tile[:].rearrange("p (t m) -> p t m", t=R), raw[:].rearrange("p (m t) -> p t m", t=R))
             return tile
 
@@ -108,10 +108,10 @@ def tile_picked_joinbonddiftop2_none_po_kernel(
 
         xs = keep.tile([P, S], U8, name="xs", align_bytes=64)
         nc.vector.tensor_copy(xs[:], xs_all[:].indirect(offs_sb[:]))
-        w1w = deal_words("w1w", w1w_raw)
+        w1w = deal_words("w1w", w1w_raw, "w1w")
         xw = keep.tile([P, S], U32, name="xw", align_bytes=64)
         nc.vector.tensor_copy(xw[:], xw_all[:].bitcast(U32).indirect(offs_sb[:]))
-        w1s = deal_scales("w1s", w1s_raw)
+        w1s = deal_scales("w1s", w1s_raw, "w1s")
 
         y_banks = []
         for t in range(R):
@@ -123,13 +123,17 @@ def tile_picked_joinbonddiftop2_none_po_kernel(
             tile = keep.tile([P, S], F32, name="y%d" % t)
             nc.scalar.copy(tile[:], y_banks[t][:])
             y.append(tile)
-        w2w = deal_words("w2w", w2w_raw)
-        w3w = deal_words("w3w", w3w_raw)
+        w2w = deal_words("w2w", w2w_raw, "w2w")
+        w3w = deal_words("w3w", w3w_raw, "w3w")
 
         neg_gy = []
-        pos_gy = [
-            keep.tile([P, R, width], F32, name="pos_gy%d" % c, tag="stage%d" % (c + 1)) for c, (c0, width) in enumerate(CHUNKS)
-        ]
+        stage = keep.tile([P, R * (W + S)], F32, name="stage")
+
+        def staged(start, width):
+            return stage[:, start : start + R * width].rearrange("p (t j) -> p t j", t=R)
+
+        pos_gy = [staged(R * (W + c0), width) for c0, width in CHUNKS]
+        z2_at = [staged(0, W), staged(R * (W + UNIT), UNIT)]
         for t in range(R):
             tile = keep.tile([P, S], F32, name="neg_gy%d" % t)
             nc.scalar.activation(tile[:], y_banks[t][:], ACT.Copy, scale=neg_gm[:, t : t + 1])
@@ -139,22 +143,26 @@ def tile_picked_joinbonddiftop2_none_po_kernel(
                     pos_gy[c][:, t, :], y_banks[t][:, c0 : c0 + width], ACT.Copy, scale=gm_sb[:, t : t + 1]
                 )
 
-        z_bf = keep.tile([P, S, R], BF16, name="z_bf", align_bytes=64)
+        z_bf = keep.tile([P, S, R], BF16, name="z_bf", tag="z_bf", align_bytes=64)
         for pair in range(R // 2):
             ts = (2 * pair, 2 * pair + 1)
-            picked = keep.tile([P, 2, 2, W], F32, name="picked%d" % pair, tag="stage0" if pair else "picked")
+            picked = z2_at[0] if pair else keep.tile([P, R, W], F32, name="picked")
             dt = {}
             for t in ts:
                 dt[t] = keep.tile([P, S], F32, name="dt%d" % t)
-                nc.vector.tensor_copy(picked[:, t % 2, 0, :], y[t][:].indirect(n1_sb[:]))
-                nc.vector.tensor_copy(picked[:, t % 2, 1, :], y[t][:].indirect(n2_sb[:]))
+                nc.vector.tensor_copy(picked[:, 2 * (t % 2), :], y[t][:].indirect(n1_sb[:]))
+                nc.vector.tensor_copy(picked[:, 2 * (t % 2) + 1, :], y[t][:].indirect(n2_sb[:]))
             for t in ts:
-                nc.vector.tensor_tensor(dt[t][:].indirect(n1_sb[:]), picked[:, t % 2, 0, :], picked[:, t % 2, 1, :], ALU.add)
+                nc.vector.tensor_tensor(
+                    dt[t][:].indirect(n1_sb[:]), picked[:, 2 * (t % 2), :], picked[:, 2 * (t % 2) + 1, :], ALU.add
+                )
             for t in ts:
-                nc.vector.tensor_tensor(dt[t][:].indirect(n2_sb[:]), picked[:, t % 2, 0, :], picked[:, t % 2, 1, :], ALU.mult)
+                nc.vector.tensor_tensor(
+                    dt[t][:].indirect(n2_sb[:]), picked[:, 2 * (t % 2), :], picked[:, 2 * (t % 2) + 1, :], ALU.mult
+                )
                 nc.scalar.activation(z_bf[:, :, t], dt[t][:], ACT.Copy, scale=gn_sb[:, t : t + 1])
-        w2s = deal_scales("w2s", w2s_raw)
-        w3s = deal_scales("w3s", w3s_raw)
+        w2s = deal_scales("w2s", w2s_raw, "w2s")
+        w3s = deal_scales("w3s", w3s_raw, "w3s")
 
         z_codes = keep.tile([P, S], U32, name="z_codes", align_bytes=64)
         z_scales = keep.tile([P, S], U8, name="z_scales", align_bytes=64)
@@ -162,7 +170,7 @@ def tile_picked_joinbonddiftop2_none_po_kernel(
         z2_scales = keep.tile([P, S], U8, name="z2_scales", align_bytes=64)
         z2_bf = []
         for c, (c0, width) in enumerate(CHUNKS):
-            z2 = keep.tile([P, R, width], F32, name="z2_%d" % c, tag="stage%d" % c)
+            z2 = z2_at[c] if c < len(z2_at) else keep.tile([P, R, width], F32, name="z2_last", tag="z_bf", align_bytes=64)[:]
             for t in range(R):
                 nc.vector.tensor_tensor(
                     z2[:, t, :],
@@ -172,9 +180,9 @@ def tile_picked_joinbonddiftop2_none_po_kernel(
                 )
             rounded = keep.tile([P, width, R], BF16, name="z2_bf%d" % c, align_bytes=64)
             if c < len(CHUNKS) - 1:
-                nc.scalar.copy(rounded[:], z2[:].rearrange("p t j -> p j t"))
+                nc.scalar.copy(rounded[:], z2.rearrange("p t j -> p j t"))
             else:
-                nc.vector.tensor_copy(rounded[:], z2[:].rearrange("p t j -> p j t"))
+                nc.vector.tensor_copy(rounded[:], z2.rearrange("p t j -> p j t"))
             z2_bf.append(rounded)
             if c == 0:
                 nc.vector.quantize_mx(z_codes[:].bitcast(FP8X4), z_scales[:], z_bf[:].rearrange("p j t -> p (j t)"))
@@ -190,15 +198,12 @@ def tile_picked_joinbonddiftop2_none_po_kernel(
             bank = psum.tile([P, S], F32, name="h_bank%d" % t, tag="bank", bufs=8)
             product(bank, w2w, w2s, t, z_codes, z_scales, True, False)
             h_banks.append(bank)
-        neg_h, pos_h = [], []
+        half_h = []
         for t in range(R):
             product(h_banks[t], w3w, w3s, t, z2_codes, z2_scales, False, True)
-            tile = keep.tile([P, S], F32, name="neg_h%d" % t)
-            nc.scalar.activation(tile[:], h_banks[t][:], ACT.Copy, scale=-1.0)
-            neg_h.append(tile)
-            tile = keep.tile([P, S], F32, name="pos_h%d" % t)
-            nc.scalar.copy(tile[:], h_banks[t][:])
-            pos_h.append(tile)
+            tile = keep.tile([P, S], F32, name="half_h%d" % t)
+            nc.scalar.activation(tile[:], h_banks[t][:], ACT.Copy, scale=0.5)
+            half_h.append(tile)
 
         out_rows = out_0.rearrange("(p t) j -> p t j", t=R)
         out_words = out_1[0].rearrange("p n t -> p (n t)").bitcast(I32)
@@ -221,52 +226,62 @@ def tile_picked_joinbonddiftop2_none_po_kernel(
                         start=(i == 0), stop=(i == len(terms) - 1), is_transpose=True,
                     )
 
+        halves = (slice(0, R // 2), slice(R // 2, R))
+        relay = keep.tile([P, R * (W + S)], F32, name="relay")
+
+        def relayed(start, width):
+            return relay[:, start : start + R * width].rearrange("p (t j) -> p t j", t=R)
+
         waiting = []
+        b1_at = 0
+        spread_tag = "spread"
         for c, (c0, width) in enumerate(CHUNKS):
             cols16 = slice(c0 // 16, (c0 + width) // 16)
-            nb1 = keep.tile([P, R, width], F32, name="nb1_%d" % c, tag="nb1")
-            nb2 = keep.tile([P, R, width], F32, name="nb2_%d" % c, tag="nb2")
-            b3 = keep.tile([P, R, width], F32, name="b3_%d" % c, tag="b3")
+            b1 = relayed(b1_at, width)
+            b1_at = R * (W + c0)
+            lead = relayed(b1_at, width)
+            step = keep.tile([P, R, width], F32, name="step%d" % c)
+            spread = keep.tile([P, R, width], F32, name="spread%d" % c, tag=spread_tag)
+            spread_tag = "extra%d" % c0
+            gap = keep.tile([P, R, width], F32, name="gap%d" % c)
+            hi = keep.tile([P, R, width], F32, name="hi%d" % c)
             for t in range(R):
-                nc.vector.tensor_copy(nb1[:, t, :], neg_h[t][:].indirect(n4_sb[:, cols16]))
-                nc.vector.tensor_copy(nb2[:, t, :], neg_h[t][:].indirect(n5_sb[:, cols16]))
-                nc.vector.tensor_copy(b3[:, t, :], pos_h[t][:].indirect(n6_sb[:, cols16]))
+                nc.vector.tensor_copy(b1[:, t, :], half_h[t][:].indirect(n4_sb[:, cols16]))
+            for t in range(R):
+                nc.vector.tensor_tensor(step[:, t, :], half_h[t][:].indirect(n5_sb[:, cols16]), b1[:, t, :], ALU.subtract)
+            nc.scalar.activation(spread[:], step[:], ACT.Abs)
+            for ts in halves:
+                nc.vector.scalar_tensor_tensor(hi[:, ts, :], step[:, ts, :], 0.0, b1[:, ts, :], ALU.max, ALU.add)
+            for t in range(R):
+                nc.vector.tensor_tensor(lead[:, t, :], half_h[t][:].indirect(n6_sb[:, cols16]), hi[:, t, :], ALU.subtract)
             for args in waiting:
                 hand_out(*args)
             waiting = []
-            for u in range(width // UNIT):
-                u0 = c0 + u * UNIT
-                cols = slice(u * UNIT, (u + 1) * UNIT)
-                neg_lo = keep.tile([P, R, UNIT], F32, name="neg_lo%d" % u0)
-                neg_hi = keep.tile([P, R, UNIT], F32, name="neg_hi%d" % u0)
-                rival = keep.tile([P, R, UNIT], F32, name="rival%d" % u0)
-                nc.vector.tensor_tensor(neg_lo[:], nb1[:, :, cols], nb2[:, :, cols], ALU.max)
-                nc.vector.tensor_tensor(neg_hi[:], nb1[:, :, cols], nb2[:, :, cols], ALU.min)
-                nc.vector.scalar_tensor_tensor(rival[:], neg_lo[:], -1.0, b3[:, :, cols], ALU.mult, ALU.max)
+            for ts in halves:
+                nc.vector.scalar_tensor_tensor(gap[:, ts, :], lead[:, ts, :], -1.0, spread[:, ts, :], ALU.mult, ALU.min)
+            for u0 in range(c0, c0 + width, UNIT):
+                cols = slice(u0 - c0, u0 - c0 + UNIT)
                 result = keep.tile([P, R, UNIT], F32, name="result%d" % u0)
                 rounded = keep.tile([P, UNIT, R], BF16, name="rounded%d" % u0, align_bytes=64)
                 if c < len(CHUNKS) - 1:
-                    hi_bank = psum.tile([P, R, UNIT], F32, name="hi_bank%d" % u0, tag="bank", bufs=8)
-                    gap_bank = psum.tile([P, R, UNIT], F32, name="gap_bank%d" % u0, tag="bank", bufs=8)
-                    sum_bank = psum.tile([P, R, UNIT], F32, name="sum_bank%d" % u0, tag="bank", bufs=8)
-                    summed_transposes(hi_bank, [neg_hi])
-                    summed_transposes(gap_bank, [neg_hi, rival])
-                    half_hi = keep.tile([P, R, UNIT], F32, name="half_hi%d" % u0)
-                    above = keep.tile([P, R, UNIT], F32, name="above%d" % u0)
-                    below = keep.tile([P, R, UNIT], F32, name="below%d" % u0)
-                    nc.scalar.activation(half_hi[:], hi_bank[:], ACT.Copy, scale=-0.5)
-                    nc.scalar.activation(above[:], gap_bank[:], ACT.Relu)
-                    nc.scalar.activation(below[:], gap_bank[:], ACT.Relu, scale=-0.5)
-                    summed_transposes(sum_bank, [half_hi, above, below])
-                    nc.scalar.copy(result[:], sum_bank[:])
-                    nc.scalar.copy(rounded[:], sum_bank[:].rearrange("p t j -> p j t"))
+                    extra = keep.tile([P, R, UNIT], F32, name="extra%d" % u0, tag="extra%d" % u0)
+                    for ts in halves:
+                        nc.scalar.activation(extra[:, ts, :], gap[:, ts, cols], ACT.Relu, scale=-3.0)
+                    turned_bank = psum.tile([P, R, UNIT], F32, name="turned_bank%d" % u0, tag="bank", bufs=8)
+                    summed_transposes(turned_bank, [hi[:, :, cols], gap[:, :, cols], extra])
+                    turned = keep.tile([P, R, UNIT], F32, name="turned%d" % u0)
+                    nc.scalar.copy(turned[:], turned_bank[:])
+                    back_bank = psum.tile([P, R, UNIT], F32, name="back_bank%d" % u0, tag="bank", bufs=8)
+                    summed_transposes(back_bank, [turned])
+                    nc.scalar.copy(rounded[:], back_bank[:].rearrange("p t j -> p j t"))
+                    nc.scalar.copy(result[:], back_bank[:])
                     waiting.append((u0, result, rounded))
                 else:
-                    first = keep.tile([P, R, UNIT], F32, name="first")
-                    second = keep.tile([P, R, UNIT], F32, name="second")
-                    nc.vector.scalar_tensor_tensor(first[:], neg_hi[:], 0.5, rival[:], ALU.mult, ALU.add)
-                    nc.vector.scalar_tensor_tensor(second[:], rival[:], -0.5, neg_hi[:], ALU.mult, ALU.subtract)
-                    nc.vector.tensor_tensor(result[:], first[:], second[:], ALU.max)
+                    bent = keep.tile([P, R, UNIT], F32, name="bent")
+                    for ts in halves:
+                        nc.vector.scalar_tensor_tensor(bent[:, ts, :], gap[:, ts, :], -2.0, gap[:, ts, :], ALU.mult, ALU.max)
+                    for ts in halves:
+                        nc.vector.tensor_tensor(result[:, ts, :], bent[:, ts, :], hi[:, ts, :], ALU.add)
                     nc.vector.tensor_copy(rounded[:], result[:].rearrange("p t j -> p j t"))
                     hand_out(u0, result, rounded)
 

from contextlib import ExitStack

import concourse.mybir as mybir
from concourse.masks import make_identity

K, T, S, N, H, W = 512, 2048, 512, 512, 512, 256
FLOPS = 2 * (K * H * S + 2 * H * N * S)

F32 = mybir.dt.float32
BF16 = mybir.dt.bfloat16
I32 = mybir.dt.int32
U32 = mybir.dt.uint32
U16 = mybir.dt.uint16
U8 = mybir.dt.uint8
FP8X4 = mybir.dt.float8_e4m3fn_x4
FP4X4 = mybir.dt.float4_e2m1fn_x4
ALU = mybir.AluOpType
ACT = mybir.ActivationFunctionType

P = 128
R = 4
CHUNKS = ((0, 256), (256, 128), (384, 128))
UNIT = 128


def tile_picked_joinbonddiftop2_none_po_kernel(
    tc, x_words, x_scales, w1_words, w1_scales, gn, gm, w2_words, w2_scales, w3_words, w3_scales,
    offs, n1, n2, n3, n4, n5, n6, out_0, out_1, out_2,
):
    nc = tc.nc
    with ExitStack() as ctx:
        lists = ctx.enter_context(tc.tile_pool(name="lists", bufs=1))
        keep = ctx.enter_context(tc.tile_pool(name="keep", bufs=1))
        psum = ctx.enter_context(tc.psum_pool(name="psum", bufs=1))

        def load_list(name, src):
            tile = lists.tile(list(src.shape), U16, name=name)
            nc.sync.dma_start(tile[:], src)
            return tile

        def load_scale_rows(queue, tile, src):
            for q in range(4):
                queue.dma_start(tile[32 * q : 32 * q + 4, :].bitcast(I32), src[0, 4 * q : 4 * q + 4, :].bitcast(I32))

        def zeroed_plane(engine, name, width):
            tile = keep.tile([P, width], U8, name=name, tag=name, align_bytes=64)
            engine.memset(tile[:].bitcast(I32), 0)
            return tile

        def load_words(name, src):
            tile = keep.tile([P, 2 * H], U8, name=name, tag=name, align_bytes=64)
            nc.sync.dma_start(tile[:].bitcast(I32), src[0].bitcast(I32))
            return tile

        def deal_words(name, raw, tag):
            tile = keep.tile([P, 2 * H], U8, name=name, tag=tag, align_bytes=64)
            nc.vector.tensor_copy(
                tile[:].rearrange("p (t m b) -> p t m b", t=R, b=2), raw[:].rearrange("p (m t b) -> p t m b", t=R, b=2)
            )
            return tile

        def deal_scales(name, raw, tag):
            tile = keep.tile([P, H], U8, name=name, tag=tag, align_bytes=64)
            nc.vector.tensor_copy(tile[:].rearrange("p (t m) -> p t m", t=R), raw[:].rearrange("p (m t) -> p t m", t=R))
            return tile

        def product(bank, words, scales, t, codes, planes, start, stop):
            nc.tensor.matmul_mx(
                out=bank[:],
                lhsT=words[:, 2 * P * t : 2 * P * (t + 1)].bitcast(FP4X4),
                lhsT_scale=scales[:, P * t : P * (t + 1)],
                rhs=codes[:].bitcast(FP8X4),
                rhs_scale=planes[:],
                start=start,
                stop=stop,
            )

        xs_all = zeroed_plane(nc.gpsimd, "xs_all", T)
        w1s_raw = zeroed_plane(nc.gpsimd, "w1s_raw", H)
        w2s_raw = zeroed_plane(nc.gpsimd, "w2s_raw", N)
        w3s_raw = zeroed_plane(nc.gpsimd, "w3s_raw", N)

        w1w_raw = load_words("w1w_raw", w1_words)
        load_scale_rows(nc.sync, xs_all, x_scales)
        offs_sb = load_list("offs_sb", offs)
        xw_all = keep.tile([P, T], I32, name="xw_all", align_bytes=64)
        nc.sync.dma_start(xw_all[:], x_words[0].rearrange("p n t -> p (n t)").bitcast(I32))
        load_scale_rows(nc.sync, w1s_raw, w1_scales)
        gm_sb = keep.tile([P, R], F32, name="gm_sb")
        nc.sync.dma_start(gm_sb[:], gm.rearrange("(p t) o -> p (t o)", t=R))
        n1_sb = load_list("n1_sb", n1)
        n2_sb = load_list("n2_sb", n2)
        w2w_raw = load_words("w2w_raw", w2_words)
        w3w_raw = load_words("w3w_raw", w3_words)
        gn_sb = keep.tile([P, R], F32, name="gn_sb")
        nc.sync.dma_start(gn_sb[:], gn.rearrange("(p t) o -> p (t o)", t=R))
        load_scale_rows(nc.sync, w2s_raw, w2_scales)
        load_scale_rows(nc.sync, w3s_raw, w3_scales)
        n3_sb = load_list("n3_sb", n3)
        n4_sb = load_list("n4_sb", n4)
        n5_sb = load_list("n5_sb", n5)
        n6_sb = load_list("n6_sb", n6)

        ident = keep.tile([P, P], F32, name="ident")
        make_identity(nc, ident[:])
        neg_gm = keep.tile([P, R], F32, name="neg_gm")
        nc.scalar.activation(neg_gm[:], gm_sb[:], ACT.Copy, scale=-1.0)

        xs = keep.tile([P, S], U8, name="xs", align_bytes=64)
        nc.vector.tensor_copy(xs[:], xs_all[:].indirect(offs_sb[:]))
        w1w = deal_words("w1w", w1w_raw, "w1w")
        xw = keep.tile([P, S], U32, name="xw", align_bytes=64)
        nc.vector.tensor_copy(xw[:], xw_all[:].bitcast(U32).indirect(offs_sb[:]))
        w1s = deal_scales("w1s", w1s_raw, "w1s")

        y_banks = []
        for t in range(R):
            bank = psum.tile([P, S], F32, name="y_bank%d" % t, tag="bank", bufs=8)
            product(bank, w1w, w1s, t, xw, xs, True, True)
            y_banks.append(bank)
        y = []
        for t in range(R):
            tile = keep.tile([P, S], F32, name="y%d" % t)
            nc.scalar.copy(tile[:], y_banks[t][:])
            y.append(tile)
        w2w = deal_words("w2w", w2w_raw, "w2w")
        w3w = deal_words("w3w", w3w_raw, "w3w")

        neg_gy = []
        stage = keep.tile([P, R * (W + S)], F32, name="stage")

        def staged(start, width):
            return stage[:, start : start + R * width].rearrange("p (t j) -> p t j", t=R)

        pos_gy = [staged(R * (W + c0), width) for c0, width in CHUNKS]
        z2_at = [staged(0, W), staged(R * (W + UNIT), UNIT)]
        for t in range(R):
            tile = keep.tile([P, S], F32, name="neg_gy%d" % t)
            nc.scalar.activation(tile[:], y_banks[t][:], ACT.Copy, scale=neg_gm[:, t : t + 1])
            neg_gy.append(tile)
            for c, (c0, width) in enumerate(CHUNKS):
                nc.scalar.activation(
                    pos_gy[c][:, t, :], y_banks[t][:, c0 : c0 + width], ACT.Copy, scale=gm_sb[:, t : t + 1]
                )

        z_bf = keep.tile([P, S, R], BF16, name="z_bf", tag="z_bf", align_bytes=64)
        for pair in range(R // 2):
            ts = (2 * pair, 2 * pair + 1)
            picked = z2_at[0] if pair else keep.tile([P, R, W], F32, name="picked")
            dt = {}
            for t in ts:
                dt[t] = keep.tile([P, S], F32, name="dt%d" % t)
                nc.vector.tensor_copy(picked[:, 2 * (t % 2), :], y[t][:].indirect(n1_sb[:]))
                nc.vector.tensor_copy(picked[:, 2 * (t % 2) + 1, :], y[t][:].indirect(n2_sb[:]))
            for t in ts:
                nc.vector.tensor_tensor(
                    dt[t][:].indirect(n1_sb[:]), picked[:, 2 * (t % 2), :], picked[:, 2 * (t % 2) + 1, :], ALU.add
                )
            for t in ts:
                nc.vector.tensor_tensor(
                    dt[t][:].indirect(n2_sb[:]), picked[:, 2 * (t % 2), :], picked[:, 2 * (t % 2) + 1, :], ALU.mult
                )
                nc.scalar.activation(z_bf[:, :, t], dt[t][:], ACT.Copy, scale=gn_sb[:, t : t + 1])
        w2s = deal_scales("w2s", w2s_raw, "w2s")
        w3s = deal_scales("w3s", w3s_raw, "w3s")

        z_codes = keep.tile([P, S], U32, name="z_codes", align_bytes=64)
        z_scales = keep.tile([P, S], U8, name="z_scales", align_bytes=64)
        z2_codes = keep.tile([P, S], U32, name="z2_codes", align_bytes=64)
        z2_scales = keep.tile([P, S], U8, name="z2_scales", align_bytes=64)
        z2_bf = []
        for c, (c0, width) in enumerate(CHUNKS):
            z2 = z2_at[c] if c < len(z2_at) else keep.tile([P, R, width], F32, name="z2_last", tag="z_bf", align_bytes=64)[:]
            for t in range(R):
                nc.vector.tensor_tensor(
                    z2[:, t, :],
                    neg_gy[t][:].indirect(n3_sb[:, c0 // 16 : (c0 + width) // 16]),
                    pos_gy[c][:, t, :],
                    ALU.add,
                )
            rounded = keep.tile([P, width, R], BF16, name="z2_bf%d" % c, align_bytes=64)
            if c < len(CHUNKS) - 1:
                nc.scalar.copy(rounded[:], z2.rearrange("p t j -> p j t"))
            else:
                nc.vector.tensor_copy(rounded[:], z2.rearrange("p t j -> p j t"))
            z2_bf.append(rounded)
            if c == 0:
                nc.vector.quantize_mx(z_codes[:].bitcast(FP8X4), z_scales[:], z_bf[:].rearrange("p j t -> p (j t)"))
        for c, (c0, width) in enumerate(CHUNKS):
            nc.vector.quantize_mx(
                z2_codes[:, c0 : c0 + width].bitcast(FP8X4),
                z2_scales[:, c0 : c0 + width],
                z2_bf[c][:].rearrange("p j t -> p (j t)"),
            )

        h_banks = []
        for t in range(R):
            bank = psum.tile([P, S], F32, name="h_bank%d" % t, tag="bank", bufs=8)
            product(bank, w2w, w2s, t, z_codes, z_scales, True, False)
            h_banks.append(bank)
        half_h = []
        for t in range(R):
            product(h_banks[t], w3w, w3s, t, z2_codes, z2_scales, False, True)
            tile = keep.tile([P, S], F32, name="half_h%d" % t)
            nc.scalar.activation(tile[:], h_banks[t][:], ACT.Copy, scale=0.5)
            half_h.append(tile)

        out_rows = out_0.rearrange("(p t) j -> p t j", t=R)
        out_words = out_1[0].rearrange("p n t -> p (n t)").bitcast(I32)
        o_codes = keep.tile([P, S], I32, name="o_codes", align_bytes=64)
        o_scales = keep.tile([P, S], U8, name="o_scales", align_bytes=64)

        def hand_out(u0, result, rounded):
            cols = slice(u0, u0 + UNIT)
            nc.sync.dma_start(out_rows[:, :, cols], result[:])
            nc.vector.quantize_mx(
                o_codes[:, cols].bitcast(FP8X4), o_scales[:, cols], rounded[:].rearrange("p j t -> p (j t)")
            )
            nc.sync.dma_start(out_words[:, cols], o_codes[:, cols])

        def summed_transposes(bank, terms):
            for t in range(R):
                for i, term in enumerate(terms):
                    nc.tensor.matmul(
                        bank[:, t, :], term[:, t, :], ident[:],
                        start=(i == 0), stop=(i == len(terms) - 1), is_transpose=True,
                    )

        halves = (slice(0, R // 2), slice(R // 2, R))
        relay = keep.tile([P, R * (W + S)], F32, name="relay")

        def relayed(start, width):
            return relay[:, start : start + R * width].rearrange("p (t j) -> p t j", t=R)

        waiting = []
        b1_at = 0
        spread_tag = "spread"
        for c, (c0, width) in enumerate(CHUNKS):
            cols16 = slice(c0 // 16, (c0 + width) // 16)
            b1 = relayed(b1_at, width)
            b1_at = R * (W + c0)
            lead = relayed(b1_at, width)
            step = keep.tile([P, R, width], F32, name="step%d" % c)
            spread = keep.tile([P, R, width], F32, name="spread%d" % c, tag=spread_tag)
            spread_tag = "extra%d" % c0
            gap = keep.tile([P, R, width], F32, name="gap%d" % c)
            hi = keep.tile([P, R, width], F32, name="hi%d" % c)
            for t in range(R):
                nc.vector.tensor_copy(b1[:, t, :], half_h[t][:].indirect(n4_sb[:, cols16]))
            for t in range(R):
                nc.vector.tensor_tensor(step[:, t, :], half_h[t][:].indirect(n5_sb[:, cols16]), b1[:, t, :], ALU.subtract)
            nc.scalar.activation(spread[:], step[:], ACT.Abs)
            for ts in halves:
                nc.vector.scalar_tensor_tensor(hi[:, ts, :], step[:, ts, :], 0.0, b1[:, ts, :], ALU.max, ALU.add)
            for t in range(R):
                nc.vector.tensor_tensor(lead[:, t, :], half_h[t][:].indirect(n6_sb[:, cols16]), hi[:, t, :], ALU.subtract)
            for args in waiting:
                hand_out(*args)
            waiting = []
            for ts in halves:
                nc.vector.scalar_tensor_tensor(gap[:, ts, :], lead[:, ts, :], -1.0, spread[:, ts, :], ALU.mult, ALU.min)
            for u0 in range(c0, c0 + width, UNIT):
                cols = slice(u0 - c0, u0 - c0 + UNIT)
                result = keep.tile([P, R, UNIT], F32, name="result%d" % u0)
                rounded = keep.tile([P, UNIT, R], BF16, name="rounded%d" % u0, align_bytes=64)
                if c < len(CHUNKS) - 1:
                    extra = keep.tile([P, R, UNIT], F32, name="extra%d" % u0, tag="extra%d" % u0)
                    for ts in halves:
                        nc.scalar.activation(extra[:, ts, :], gap[:, ts, cols], ACT.Relu, scale=-3.0)
                    turned_bank = psum.tile([P, R, UNIT], F32, name="turned_bank%d" % u0, tag="bank", bufs=8)
                    summed_transposes(turned_bank, [hi[:, :, cols], gap[:, :, cols], extra])
                    turned = keep.tile([P, R, UNIT], F32, name="turned%d" % u0)
                    nc.scalar.copy(turned[:], turned_bank[:])
                    back_bank = psum.tile([P, R, UNIT], F32, name="back_bank%d" % u0, tag="bank", bufs=8)
                    summed_transposes(back_bank, [turned])
                    nc.scalar.copy(rounded[:], back_bank[:].rearrange("p t j -> p j t"))
                    nc.scalar.copy(result[:], back_bank[:])
                    waiting.append((u0, result, rounded))
                else:
                    bent = keep.tile([P, R, UNIT], F32, name="bent")
                    for ts in halves:
                        nc.vector.scalar_tensor_tensor(bent[:, ts, :], gap[:, ts, :], -2.0, gap[:, ts, :], ALU.mult, ALU.max)
                    for ts in halves:
                        nc.vector.tensor_tensor(result[:, ts, :], bent[:, ts, :], hi[:, ts, :], ALU.add)
                    nc.vector.tensor_copy(rounded[:], result[:].rearrange("p t j -> p j t"))
                    hand_out(u0, result, rounded)

        for q in range(4):
            queue = nc.scalar if q % 2 else nc.sync
            queue.dma_start(out_2[0, 4 * q : 4 * q + 4, :].bitcast(I32), o_scales[32 * q : 32 * q + 4, :].bitcast(I32))
